import numpy as np
import ml_dtypes


def mxq(x, axis, fmt="e4m3"):
    dtype, down = {"e4m3": (ml_dtypes.float8_e4m3fn, 7), "e5m2": (ml_dtypes.float8_e5m2, 14)}[fmt]
    v = np.moveaxis(np.asarray(x, np.float32).astype(ml_dtypes.bfloat16).astype(np.float64), axis, -1)
    blocks = v.reshape(v.shape[:-1] + (-1, 32))
    amax = np.abs(blocks).max(-1, keepdims=True)
    byte = np.maximum(np.where(amax > 0, np.frexp(amax)[1] - 1 + 127, 0) - down, 1)
    scale = np.exp2(byte - 127.0)
    codes = (blocks / scale).astype(np.float32).astype(dtype).astype(np.float64)
    return np.moveaxis((codes * scale).reshape(v.shape), -1, axis)


WIDE = False


def mx_kscale(k):
    if not WIDE:
        return np.ones(k)
    levels = np.array([10, -10, 5, -5, 0])
    if k % 512:
        return np.exp2(np.random.permutation(np.resize(levels, k // 32))).repeat(32)
    a = np.empty((k // 512, 16))
    for p in range(k // 512):
        a[p, :8] = np.random.permutation(np.resize(levels, 8))
        for g in range(8):
            far = levels[np.abs(levels - a[p, g]) >= 10]
            a[p, g + 8] = far[np.random.randint(len(far))]
    return np.exp2(a.ravel()).repeat(32)


def f64(x):
    return np.asarray(x).astype(np.float64)


def striped(idx):
    return np.tile(idx.reshape(-1, 16).T, (8, 1)).astype(np.uint16)


def unstriped(offs):
    return offs[:16].T.reshape(-1).astype(np.int64)


def pack_weight(w):
    k, n = w.shape
    w = f64(np.asarray(w, np.float32).astype(ml_dtypes.bfloat16)).reshape(k // 32, 32, n)
    amax = np.abs(w).max(1)
    byte = np.clip(np.where(amax > 0, np.frexp(amax)[1] - 1 + 127 - 7, 1), 1, 254)
    scaled = (w * np.exp2(127.0 - byte)[:, None, :]).reshape(k, n).astype(np.float32)
    words = np.ascontiguousarray(scaled.reshape(k // 512, 128, 4, n).transpose(0, 1, 3, 2)).astype(ml_dtypes.float8_e4m3fn).view(np.uint8)
    return words, np.ascontiguousarray(byte.astype(np.uint8).reshape(k // 512, 16, n))


def unpack_weight(words, scales):
    g, p, n, _ = words.shape
    vals = np.ascontiguousarray(words).view(ml_dtypes.float8_e4m3fn).astype(np.float64) * np.repeat(np.exp2(scales.astype(np.float64) - 127.0), 8, axis=1)[..., None]
    return vals.transpose(0, 1, 3, 2).reshape(g * 512, n)


E2M1 = np.array([0.0, 0.5, 1.0, 1.5, 2.0, 3.0, 4.0, 6.0, -0.0, -0.5, -1.0, -1.5, -2.0, -3.0, -4.0, -6.0])


def pack_fp4(w):
    k, n = w.shape
    w = f64(np.asarray(w, np.float32).astype(ml_dtypes.bfloat16)).reshape(k // 32, 32, n)
    amax = np.abs(w).max(1)
    mant, ex = np.frexp(amax / 6.0)
    byte = np.clip(np.where(amax > 0, np.where(mant > 0.5, ex, ex - 1) + 127, 1), 1, 254)
    scaled = (w * np.exp2(127.0 - byte)[:, None, :]).reshape(k, n).astype(np.float32)
    c = np.ascontiguousarray(scaled.reshape(k // 512, 128, 4, n).transpose(0, 1, 3, 2)).astype(ml_dtypes.float4_e2m1fn).view(np.uint8) & 0xF
    words = (c[..., 0::2] | (c[..., 1::2] << 4)).reshape(k // 512, 128, 2 * n)
    return np.ascontiguousarray(words), np.ascontiguousarray(byte.astype(np.uint8).reshape(k // 512, 16, n))


def unpack_fp4(words, scales):
    g, _, n = scales.shape
    words = np.ascontiguousarray(words).reshape(g, 128, n, 2)
    nib = np.empty((g, 128, n, 4), np.uint8)
    nib[..., 0::2] = words & 0xF
    nib[..., 1::2] = words >> 4
    vals = E2M1[nib] * np.repeat(np.exp2(scales.astype(np.float64) - 127.0), 8, axis=1)[..., None]
    return vals.transpose(0, 1, 3, 2).reshape(g * 512, n)


def gelu(v):
    return 0.5 * v * (1.0 + np.tanh(np.sqrt(2.0 / np.pi) * (v + 0.044715 * v**3)))


K, T, S, H, N = 512, 2048, 1024, 512, 128
P = 2 ** 7


def setup_inputs():
    n = np.random.standard_normal
    s = mx_kscale(K)[:, None]
    u = mx_kscale(H)
    packed_xT = pack_weight(n((K, T)) * s)
    packed_w2 = pack_fp4(n((H, N)) / np.sqrt(H) / u[:, None])
    return {
        "x_words": packed_xT[0],
        "x_scales": packed_xT[1],
        "w1": (n((K, H)) / np.sqrt(K) / s * u).astype(np.float32),
        "w2_words": packed_w2[0],
        "w2_scales": packed_w2[1],
        "lam": np.tile(np.random.uniform(0.1, 0.9, S), (P, 1)).astype(np.float32),
        "mu": np.tile(np.random.uniform(0.1, 0.9, S), (P, 1)).astype(np.float32),
        "offs": striped(np.random.permutation(T)[:S]),
        "pos1": striped(np.random.permutation(S)),
    }


def reference(x_words, x_scales, w1, w2_words, w2_scales, lam, mu, offs, pos1):
    xq = unpack_weight(x_words, x_scales)[:, unstriped(offs)]
    h = gelu(mxq(f64(w1), 0, "e4m3").T @ xq)
    z = h * f64(lam)[:1] + h[:, unstriped(pos1)] * f64(mu)[:1]
    return unpack_fp4(w2_words, w2_scales).T @ mxq(z, 0, "e4m3")

@@ -1,0 +1,221 @@
+from contextlib import ExitStack
+
+import concourse.mybir as mybir
+from concourse.masks import make_identity
+
+K, T, S, H, N = 512, 2048, 1024, 512, 128
+FLOPS = 2 * K * H * S + 2 * H * N * S
+
+F32 = mybir.dt.float32
+BF16 = mybir.dt.bfloat16
+I32 = mybir.dt.int32
+U32 = mybir.dt.uint32
+U16 = mybir.dt.uint16
+U8 = mybir.dt.uint8
+FP8X4 = mybir.dt.float8_e4m3fn_x4
+FP4X4 = mybir.dt.float4_e2m1fn_x4
+GELU = mybir.ActivationFunctionType.Gelu_apprx_tanh
+COPY = mybir.ActivationFunctionType.Copy
+MULT = mybir.AluOpType.mult
+ADD = mybir.AluOpType.add
+
+P = 128
+PACK = 4
+HALF = 512
+BLOCKS = S // P
+GROUPS = [(0, 1), (2, 3), (4, 5), (6,), (7,)]
+
+
+def tile_picked_mixup_gelu_p_kernel(
+    tc, x_words, x_scales, w1, w2_words, w2_scales, lam, mu, offs, pos1, out
+):
+    nc = tc.nc
+    with ExitStack() as ctx:
+        keep = ctx.enter_context(tc.tile_pool(name="keep", bufs=1))
+        psum = ctx.enter_context(tc.psum_pool(name="psum", bufs=1))
+
+        def bank(i, name):
+            return psum.tile([P, 512], F32, name=name, tag="bank%d" % i)
+
+        offs_t = keep.tile([P, S // 16], U16, name="offs_t")
+        nc.sync.dma_start(offs_t[:], offs)
+
+        xs = keep.tile([P, T], U8, name="xs", align_bytes=64)
+        nc.vector.memset(xs[:, : T // 2].bitcast(I32), 0)
+        nc.gpsimd.memset(xs[:, T // 2 :].bitcast(I32), 0)
+        for q in range(4):
+            nc.sync.dma_start(
+                xs[32 * q : 32 * q + 4, :].bitcast(I32),
+                x_scales[0, 4 * q : 4 * q + 4, :].bitcast(I32),
+            )
+        xw = keep.tile([P, T], I32, name="xw", align_bytes=64)
+        nc.sync.dma_start(xw[:], x_words[0].rearrange("p n t -> p (n t)").bitcast(I32))
+
+        w1_rows = w1.rearrange("(p j) c -> p j c", j=PACK)
+
+        def load_w1(first, count):
+            raw = keep.tile([P, PACK, P * count], F32, name="w1_raw%d" % first, align_bytes=64)
+            nc.sync.dma_start(raw[:], w1_rows[:, :, P * first : P * (first + count)])
+            return raw
+
+        raw0, raw1, raw23 = load_w1(0, 1), load_w1(1, 1), load_w1(2, 2)
+        pos_t = keep.tile([P, S // 16], U16, name="pos_t")
+        nc.sync.dma_start(pos_t[:], pos1)
+
+        ident = keep.tile([P, P], F32, name="ident", align_bytes=64)
+        make_identity(nc, ident[:])
+        warm = keep.tile([P, 2], F32, name="warm")
+        nc.scalar.activation(warm[:], ident[:, 0:2], GELU)
+
+        share_rows = keep.tile([P, P], F32, name="share_rows", align_bytes=64)
+        nc.gpsimd.memset(share_rows[:], 0.0)
+        w2s = keep.tile([P, N], U8, name="w2s", align_bytes=64)
+        nc.gpsimd.memset(w2s[:].bitcast(I32), 0)
+        nc.scalar.dma_start(share_rows[0:8, :], lam[0].rearrange("(b p) -> b p", p=P))
+        nc.scalar.dma_start(share_rows[8:16, :], mu[0].rearrange("(b p) -> b p", p=P))
+        w2w = keep.tile([P, 2 * N], U8, name="w2w", align_bytes=64)
+        nc.sync.dma_start(w2w[:].bitcast(I32), w2_words[0].bitcast(I32))
+        for q in range(4):
+            nc.sync.dma_start(
+                w2s[32 * q : 32 * q + 4, :].bitcast(I32),
+                w2_scales[0, 4 * q : 4 * q + 4, :].bitcast(I32),
+            )
+
+        xs_g = keep.tile([P, S], U8, name="xs_g", align_bytes=64)
+        nc.vector.tensor_copy(xs_g[:], xs[:].indirect(offs_t[:]))
+
+        def gather_words(dst, lo, n):
+            nc.vector.tensor_copy(dst, xw[:].bitcast(U32).indirect(offs_t[:, lo // 16 : (lo + n) // 16]))
+            return dst
+
+        def quantize(grouped_flat, width, name):
+            codes = keep.tile([P, width], U32, name=name + "_codes", align_bytes=64)
+            scales = keep.tile([P, width], U8, name=name + "_scales", align_bytes=64)
+            nc.vector.quantize_mx(out=codes[:].bitcast(FP8X4), scales=scales[:], in_=grouped_flat)
+            return codes, scales
+
+        def group_w1(copy, raw, first, count):
+            grouped = keep.tile([P, count * P * PACK], BF16, name="w1_grouped%d" % first, tag="w1_grouped%d" % first, align_bytes=64)
+            copy(grouped[:].rearrange("p (c j) -> p c j", j=PACK), raw[:].rearrange("p j c -> p c j"))
+            return grouped
+
+        pieces = [(0, 512), (512, 256), (768, 256)]
+        xw_a = keep.tile([P, HALF], U32, name="xw_a", align_bytes=64)
+        xw_g = [gather_words(xw_a[:], 0, 512)]
+        grouped0 = group_w1(nc.scalar.copy, raw0, 0, 1)
+        q0 = quantize(grouped0[:], P, "w1_0")
+        xw_b = keep.tile([P, HALF], U32, name="xw_b", tag="w1_grouped0", align_bytes=64)
+        xw_g.append(gather_words(xw_b[:, :256], 512, 256))
+        xw_g.append(gather_words(xw_b[:, 256:], 768, 256))
+        q1 = quantize(group_w1(nc.scalar.copy, raw1, 1, 1)[:], P, "w1_1")
+        q23 = quantize(group_w1(nc.vector.tensor_copy, raw23, 2, 2)[:], 2 * P, "w1_2")
+        w1q = [(q0[0][:], q0[1][:]), (q1[0][:], q1[1][:])]
+        w1q.extend([(q23[0][:, P * i : P * (i + 1)], q23[1][:, P * i : P * (i + 1)]) for i in range(2)])
+
+        def cols(bk, c):
+            return bk[:].rearrange("p (u c m e) -> p c m u e", u=2, c=4, e=2)[:, c]
+
+        h = []
+        g = {}
+        g_tag = {}
+        steps = [(0, [0]), (0, [1]), (0, [2])] + [(c, ids) for c in range(1, 4) for ids in ([0], [1, 2])]
+        for c in range(4):
+            h.append(keep.tile([P, S], F32, name="h%d" % c, tag="h%d" % c, align_bytes=64))
+        for k, (c, ids) in enumerate(steps):
+            acc = bank(k % 4, "acc%d_%d" % (c, ids[0]))
+            first = pieces[ids[0]][0]
+            width = sum(pieces[i][1] for i in ids)
+            for i in ids:
+                lo, n = pieces[i]
+                nc.tensor.matmul_mx(
+                    out=acc[:, lo - first : lo - first + n],
+                    lhsT=w1q[c][0].bitcast(FP8X4),
+                    lhsT_scale=w1q[c][1],
+                    rhs=xw_g[i].bitcast(FP8X4),
+                    rhs_scale=xs_g[:, lo : lo + n],
+                    start=True,
+                    stop=True,
+                )
+            nc.scalar.activation(h[c][:, first : first + width], acc[:, :width], GELU)
+
+        def bank_of(b):
+            return (b + 4) % 8 if b < 4 else (b - 3) % 4
+
+        share_ps = bank(7, "share_ps")
+        nc.tensor.transpose(share_ps[:, 0:P], share_rows[:], ident[:])
+        shares = keep.tile([P, 16], F32, name="shares")
+        nc.scalar.copy(shares[:], share_ps[:, 0:16])
+
+        hT = [bank(bank_of(b), "hT%d" % b) for b in range(BLOCKS)]
+        for b in range(BLOCKS):
+            for c in range(4):
+                nc.tensor.transpose(cols(hT[b], c), h[c][:, P * b : P * (b + 1)], ident[:])
+
+        def gather_h(c, hf):
+            name = "g%d_%d" % (c, hf)
+            gt = keep.tile([P, HALF], F32, name=name, tag=g_tag.get((c, hf), name), align_bytes=64)
+            nc.vector.tensor_copy(gt[:], h[c][:].indirect(pos_t[:, 32 * hf : 32 * (hf + 1)]))
+            g[c, hf] = gt
+
+        own = []
+        for b in range(BLOCKS):
+            a = keep.tile([P, H], F32, name="own%d" % b, align_bytes=64)
+            nc.scalar.activation(a[:], hT[b][:], COPY, scale=shares[:, b : b + 1])
+            own.append(a)
+
+        gT = [bank(bank_of(b), "gT%d" % b) for b in range(BLOCKS)]
+        for c in range(4):
+            for hf in range(2):
+                gather_h(c, hf)
+                for b in range(4 * hf, 4 * hf + 4):
+                    src = g[c, hf][:, P * (b % 4) : P * (b % 4 + 1)]
+                    nc.tensor.transpose(cols(gT[b], c), src, ident[:])
+
+        zT = {}
+
+        def mix(b):
+            z = keep.tile([P, H], BF16, name="zT%d" % b, align_bytes=64)
+            nc.vector.scalar_tensor_tensor(z[:], gT[b][:], shares[:, 8 + b : 9 + b], own[b][:], MULT, ADD)
+            zT[b] = z
+
+        def turn(grp):
+            n = P * len(grp)
+            wb = bank(bank_of(grp[0]), "words%d" % grp[0])
+            for i, b in enumerate(grp):
+                words = zT[b][:].bitcast(F32)
+                for u in range(2):
+                    nc.tensor.transpose(
+                        wb[:, 256 * i + P * u : 256 * i + P * (u + 1)], words[:, P * u : P * (u + 1)], ident[:]
+                    )
+            zg = keep.tile([P, n, PACK], BF16, name="zg%d" % grp[0], align_bytes=64)
+            dst = zg[:].rearrange("p s t -> p (s t)").bitcast(F32).rearrange("p (i s u) -> p i s u", u=2, s=P)
+            nc.scalar.copy(dst, wb[:, 0 : 2 * n].rearrange("p (i u s) -> p i s u", u=2, s=P))
+            return zg
+
+        def finish(grp, zg, ob):
+            n = P * len(grp)
+            codes, scales = quantize(zg[:].rearrange("p s t -> p (s t)"), n, "z%d" % grp[0])
+            acc = bank(ob, "out%d" % grp[0])
+            nc.tensor.matmul_mx(
+                out=acc[:, 0:n],
+                lhsT=w2w[:].bitcast(FP4X4),
+                lhsT_scale=w2s[:],
+                rhs=codes[:].bitcast(FP8X4),
+                rhs_scale=scales[:],
+                start=True,
+                stop=True,
+            )
+            res = keep.tile([P, n], F32, name="res%d" % grp[0], align_bytes=64)
+            nc.scalar.copy(res[:], acc[:, 0:n])
+            nc.sync.dma_start(out[:, P * grp[0] : P * grp[0] + n], res[:])
+
+        out_banks = [5, 7, 2, 4, 6]
+        pending = None
+        for gi, grp in enumerate(GROUPS):
+            for b in grp:
+                mix(b)
+            zg = turn(grp)
+            if pending is not None:
+                finish(*pending)
+            pending = (grp, zg, out_banks[gi])
+        finish(*pending)

@@ -40,17 +40,6 @@ def tile_picked_mixup_gelu_p_kernel(
         offs_t = keep.tile([P, S // 16], U16, name="offs_t")
         nc.sync.dma_start(offs_t[:], offs)
 
-        xs = keep.tile([P, T], U8, name="xs", align_bytes=64)
-        nc.vector.memset(xs[:, : T // 2].bitcast(I32), 0)
-        nc.gpsimd.memset(xs[:, T // 2 :].bitcast(I32), 0)
-        for q in range(4):
-            nc.sync.dma_start(
-                xs[32 * q : 32 * q + 4, :].bitcast(I32),
-                x_scales[0, 4 * q : 4 * q + 4, :].bitcast(I32),
-            )
-        xw = keep.tile([P, T], I32, name="xw", align_bytes=64)
-        nc.sync.dma_start(xw[:], x_words[0].rearrange("p n t -> p (n t)").bitcast(I32))
-
         w1_rows = w1.rearrange("(p j) c -> p j c", j=PACK)
 
         def load_w1(first, count):
@@ -58,7 +47,20 @@ def tile_picked_mixup_gelu_p_kernel(
             nc.sync.dma_start(raw[:], w1_rows[:, :, P * first : P * (first + count)])
             return raw
 
-        raw0, raw1, raw23 = load_w1(0, 1), load_w1(1, 1), load_w1(2, 2)
+
+        xs = keep.tile([P, T], U8, name="xs", tag="xs", align_bytes=64)
+        nc.vector.memset(xs[:, : T // 2].bitcast(I32), 0)
+        nc.gpsimd.memset(xs[:, T // 2 :].bitcast(I32), 0)
+        for q in range(4):
+            (nc.sync if q < 2 else nc.scalar).dma_start(
+                xs[32 * q : 32 * q + 4, :].bitcast(I32),
+                x_scales[0, 4 * q : 4 * q + 4, :].bitcast(I32),
+            )
+
+        raw0 = load_w1(0, 1)
+        xw = keep.tile([P, T], I32, name="xw", align_bytes=64)
+        nc.sync.dma_start(xw[:], x_words[0].rearrange("p n t -> p (n t)").bitcast(I32))
+        raw1, raw23 = load_w1(1, 1), load_w1(2, 2)
         pos_t = keep.tile([P, S // 16], U16, name="pos_t")
         nc.sync.dma_start(pos_t[:], pos1)
 
@@ -71,8 +73,8 @@ def tile_picked_mixup_gelu_p_kernel(
         nc.gpsimd.memset(share_rows[:], 0.0)
         w2s = keep.tile([P, N], U8, name="w2s", align_bytes=64)
         nc.gpsimd.memset(w2s[:].bitcast(I32), 0)
-        nc.scalar.dma_start(share_rows[0:8, :], lam[0].rearrange("(b p) -> b p", p=P))
-        nc.scalar.dma_start(share_rows[8:16, :], mu[0].rearrange("(b p) -> b p", p=P))
+        nc.sync.dma_start(share_rows[0:8, :], lam[0].rearrange("(b p) -> b p", p=P))
+        nc.sync.dma_start(share_rows[8:16, :], mu[0].rearrange("(b p) -> b p", p=P))
         w2w = keep.tile([P, 2 * N], U8, name="w2w", align_bytes=64)
         nc.sync.dma_start(w2w[:].bitcast(I32), w2_words[0].bitcast(I32))
         for q in range(4):
@@ -89,31 +91,40 @@ def tile_picked_mixup_gelu_p_kernel(
             return dst
 
         def quantize(grouped_flat, width, name):
-            codes = keep.tile([P, width], U32, name=name + "_codes", align_bytes=64)
+            codes = keep.tile([P, width], U32, name=name + "_codes", tag={"z0": "own7"}.get(name, name), align_bytes=64)
             scales = keep.tile([P, width], U8, name=name + "_scales", align_bytes=64)
             nc.vector.quantize_mx(out=codes[:].bitcast(FP8X4), scales=scales[:], in_=grouped_flat)
             return codes, scales
 
-        def group_w1(copy, raw, first, count):
-            grouped = keep.tile([P, count * P * PACK], BF16, name="w1_grouped%d" % first, tag="w1_grouped%d" % first, align_bytes=64)
-            copy(grouped[:].rearrange("p (c j) -> p c j", j=PACK), raw[:].rearrange("p j c -> p c j"))
+        def group_w1(copy, raw, c):
+            grouped = keep.tile([P, raw.shape[2] * PACK], BF16, name="w1_grouped%d" % c, align_bytes=64)
+            copy(
+                grouped[:].rearrange("p (u m e j) -> p m j u e", u=2, e=2, j=PACK),
+                raw.rearrange("p j (m u e) -> p m j u e", u=2, e=2),
+            )
             return grouped
 
         pieces = [(0, 512), (512, 256), (768, 256)]
         xw_a = keep.tile([P, HALF], U32, name="xw_a", align_bytes=64)
         xw_g = [gather_words(xw_a[:], 0, 512)]
-        grouped0 = group_w1(nc.scalar.copy, raw0, 0, 1)
+        grouped0 = group_w1(nc.scalar.copy, raw0[:], 0)
         q0 = quantize(grouped0[:], P, "w1_0")
-        xw_b = keep.tile([P, HALF], U32, name="xw_b", tag="w1_grouped0", align_bytes=64)
+        xw_b = keep.tile([P, HALF], U32, name="xw_b", align_bytes=64)
         xw_g.append(gather_words(xw_b[:, :256], 512, 256))
         xw_g.append(gather_words(xw_b[:, 256:], 768, 256))
-        q1 = quantize(group_w1(nc.scalar.copy, raw1, 1, 1)[:], P, "w1_1")
-        q23 = quantize(group_w1(nc.vector.tensor_copy, raw23, 2, 2)[:], 2 * P, "w1_2")
-        w1q = [(q0[0][:], q0[1][:]), (q1[0][:], q1[1][:])]
-        w1q.extend([(q23[0][:, P * i : P * (i + 1)], q23[1][:, P * i : P * (i + 1)]) for i in range(2)])
+        q1 = quantize(group_w1(nc.scalar.copy, raw1[:], 1)[:], P, "w1_1")
+        q23 = quantize(group_w1(nc.vector.tensor_copy, raw23[:], 2)[:], 2 * P, "w1_2")
+        w1q = [q0, q1] + [(q23[0][:, P * u : P * (u + 1)], q23[1][:, P * u : P * (u + 1)]) for u in range(2)]
+
+        share_ps = bank(7, "share_ps")
+        nc.tensor.transpose(share_ps[:, 0:P], share_rows[:], ident[:])
+        shares = keep.tile([P, 16], F32, name="shares")
+        nc.scalar.copy(shares[:], share_ps[:, 0:16])
 
         def cols(bk, c):
-            return bk[:].rearrange("p (u c m e) -> p c m u e", u=2, c=4, e=2)[:, c]
+            if c < 2:
+                return bk[:].rearrange("p (u c r) -> p c u r", u=2, c=4)[:, c]
+            return bk[:, 256 * (c - 2) + P : 256 * (c - 1)]
 
         h = []
         g = {}
@@ -129,8 +140,8 @@ def tile_picked_mixup_gelu_p_kernel(
                 lo, n = pieces[i]
                 nc.tensor.matmul_mx(
                     out=acc[:, lo - first : lo - first + n],
-                    lhsT=w1q[c][0].bitcast(FP8X4),
-                    lhsT_scale=w1q[c][1],
+                    lhsT=w1q[c][0][:].bitcast(FP8X4),
+                    lhsT_scale=w1q[c][1][:],
                     rhs=xw_g[i].bitcast(FP8X4),
                     rhs_scale=xs_g[:, lo : lo + n],
                     start=True,
@@ -140,11 +151,6 @@ def tile_picked_mixup_gelu_p_kernel(
 
         def bank_of(b):
             return (b + 4) % 8 if b < 4 else (b - 3) % 4
-
-        share_ps = bank(7, "share_ps")
-        nc.tensor.transpose(share_ps[:, 0:P], share_rows[:], ident[:])
-        shares = keep.tile([P, 16], F32, name="shares")
-        nc.scalar.copy(shares[:], share_ps[:, 0:16])
 
         hT = [bank(bank_of(b), "hT%d" % b) for b in range(BLOCKS)]
         for b in range(BLOCKS):
@@ -159,7 +165,7 @@ def tile_picked_mixup_gelu_p_kernel(
 
         own = []
         for b in range(BLOCKS):
-            a = keep.tile([P, H], F32, name="own%d" % b, align_bytes=64)
+            a = keep.tile([P, H], F32, name="own%d" % b, tag="own%d" % b, align_bytes=64)
             nc.scalar.activation(a[:], hT[b][:], COPY, scale=shares[:, b : b + 1])
             own.append(a)
 
@@ -210,12 +216,10 @@ def tile_picked_mixup_gelu_p_kernel(
             nc.sync.dma_start(out[:, P * grp[0] : P * grp[0] + n], res[:])
 
         out_banks = [5, 7, 2, 4, 6]
-        pending = None
-        for gi, grp in enumerate(GROUPS):
+        turned = []
+        for grp in GROUPS:
             for b in grp:
                 mix(b)
-            zg = turn(grp)
-            if pending is not None:
-                finish(*pending)
-            pending = (grp, zg, out_banks[gi])
-        finish(*pending)
+            turned.append(turn(grp))
+        for grp, zg, ob in zip(GROUPS, turned, out_banks):
+            finish(grp, zg, ob)

@@ -23,6 +23,8 @@ P = 128
 PACK = 4
 HALF = 512
 BLOCKS = S // P
+ACC_BANK = [0,1,2,3,0,1,2,3,0]
+BLOCK_BANK = [4,5,6,7,1,2,3,0]
 GROUPS = [(0, 1), (2, 3), (4, 5), (6,), (7,)]
 
 
@@ -42,9 +44,9 @@ def tile_picked_mixup_gelu_p_kernel(
 
         w1_rows = w1.rearrange("(p j) c -> p j c", j=PACK)
 
-        def load_w1(first, count):
+        def load_w1(first, count, queue=nc.sync):
             raw = keep.tile([P, PACK, P * count], F32, name="w1_raw%d" % first, align_bytes=64)
-            nc.sync.dma_start(raw[:], w1_rows[:, :, P * first : P * (first + count)])
+            queue.dma_start(raw[:], w1_rows[:, :, P * first : P * (first + count)])
             return raw
 
 
@@ -57,7 +59,7 @@ def tile_picked_mixup_gelu_p_kernel(
                 x_scales[0, 4 * q : 4 * q + 4, :].bitcast(I32),
             )
 
-        raw0 = load_w1(0, 1)
+        raw0 = load_w1(0, 1, nc.scalar)
         xw = keep.tile([P, T], I32, name="xw", align_bytes=64)
         nc.sync.dma_start(xw[:], x_words[0].rearrange("p n t -> p (n t)").bitcast(I32))
         raw1, raw23 = load_w1(1, 1), load_w1(2, 2)
@@ -91,7 +93,7 @@ def tile_picked_mixup_gelu_p_kernel(
             return dst
 
         def quantize(grouped_flat, width, name):
-            codes = keep.tile([P, width], U32, name=name + "_codes", tag={"z0": "own7"}.get(name, name), align_bytes=64)
+            codes = keep.tile([P, width], U32, name=name + "_codes", align_bytes=64)
             scales = keep.tile([P, width], U8, name=name + "_scales", align_bytes=64)
             nc.vector.quantize_mx(out=codes[:].bitcast(FP8X4), scales=scales[:], in_=grouped_flat)
             return codes, scales
@@ -133,7 +135,7 @@ def tile_picked_mixup_gelu_p_kernel(
         for c in range(4):
             h.append(keep.tile([P, S], F32, name="h%d" % c, tag="h%d" % c, align_bytes=64))
         for k, (c, ids) in enumerate(steps):
-            acc = bank(k % 4, "acc%d_%d" % (c, ids[0]))
+            acc = bank(ACC_BANK[k], "acc%d_%d" % (c, ids[0]))
             first = pieces[ids[0]][0]
             width = sum(pieces[i][1] for i in ids)
             for i in ids:
@@ -150,12 +152,18 @@ def tile_picked_mixup_gelu_p_kernel(
             nc.scalar.activation(h[c][:, first : first + width], acc[:, :width], GELU)
 
         def bank_of(b):
-            return (b + 4) % 8 if b < 4 else (b - 3) % 4
+            return BLOCK_BANK[b]
 
         hT = [bank(bank_of(b), "hT%d" % b) for b in range(BLOCKS)]
-        for b in range(BLOCKS):
-            for c in range(4):
-                nc.tensor.transpose(cols(hT[b], c), h[c][:, P * b : P * (b + 1)], ident[:])
+        def ready_step(c, b):
+            made = max(k for k, (cc, ids) in enumerate(steps) if cc == c and pieces[ids[0]][0] <= P * b)
+            freed = max([k for k in range(len(steps)) if ACC_BANK[k] == bank_of(b)] + [0])
+            return max(made, freed)
+
+        order = sorted((ready_step(c, b), b, c) for b in range(BLOCKS) for c in range(4))
+        order = [(c, b) for step, b, c in order]
+        for c, b in order:
+            nc.tensor.transpose(cols(hT[b], c), h[c][:, P * b : P * (b + 1)], ident[:])
 
         def gather_h(c, hf):
             name = "g%d_%d" % (c, hf)
@@ -173,9 +181,15 @@ def tile_picked_mixup_gelu_p_kernel(
         for c in range(4):
             for hf in range(2):
                 gather_h(c, hf)
-                for b in range(4 * hf, 4 * hf + 4):
-                    src = g[c, hf][:, P * (b % 4) : P * (b % 4 + 1)]
-                    nc.tensor.transpose(cols(gT[b], c), src, ident[:])
+
+        def turn_g(c, b):
+            nc.tensor.transpose(cols(gT[b], c), g[c, b // 4][:, P * (b % 4) : P * (b % 4 + 1)], ident[:])
+
+        order = [(c, b) for b in range(4) for c in range(2)] + [(2, b) for b in range(4)]
+        order = order + [(c, b) for b in range(4, 7) for c in range(3)] + [(3, b) for b in range(4)]
+        order = order + [(c, 7) for c in range(3)] + [(3, b) for b in range(4, 8)]
+        for c, b in order:
+            turn_g(c, b)
 
         zT = {}
 
@@ -212,10 +226,10 @@ def tile_picked_mixup_gelu_p_kernel(
                 stop=True,
             )
             res = keep.tile([P, n], F32, name="res%d" % grp[0], align_bytes=64)
-            nc.scalar.copy(res[:], acc[:, 0:n])
+            (nc.vector.tensor_copy if grp[0] == 7 else nc.scalar.copy)(res[:], acc[:, 0:n])
             nc.sync.dma_start(out[:, P * grp[0] : P * grp[0] + n], res[:])
 
-        out_banks = [5, 7, 2, 4, 6]
+        out_banks = [bank_of(1), bank_of(3), bank_of(5), bank_of(0), bank_of(2)]
         turned = []
         for grp in GROUPS:
             for b in grp:

@@ -44,9 +44,9 @@ def tile_picked_mixup_gelu_p_kernel(
 
         w1_rows = w1.rearrange("(p j) c -> p j c", j=PACK)
 
-        def load_w1(first, count, queue=nc.sync):
+        def load_w1(first, count):
             raw = keep.tile([P, PACK, P * count], F32, name="w1_raw%d" % first, align_bytes=64)
-            queue.dma_start(raw[:], w1_rows[:, :, P * first : P * (first + count)])
+            nc.sync.dma_start(raw[:], w1_rows[:, :, P * first : P * (first + count)])
             return raw
 
 
@@ -59,7 +59,7 @@ def tile_picked_mixup_gelu_p_kernel(
                 x_scales[0, 4 * q : 4 * q + 4, :].bitcast(I32),
             )
 
-        raw0 = load_w1(0, 1, nc.scalar)
+        raw0 = load_w1(0, 1)
         xw = keep.tile([P, T], I32, name="xw", align_bytes=64)
         nc.sync.dma_start(xw[:], x_words[0].rearrange("p n t -> p (n t)").bitcast(I32))
         raw1, raw23 = load_w1(1, 1), load_w1(2, 2)

@@ -21,11 +21,16 @@ ADD = mybir.AluOpType.add
 
 P = 128
 PACK = 4
-HALF = 512
+ALIGN = 64
+BANK = 512
+HALF = S // 2
+PER_COLUMN = 16
+TILES = H // P
 BLOCKS = S // P
-ACC_BANK = [0,1,2,3,0,1,2,3,0]
-BLOCK_BANK = [4,5,6,7,1,2,3,0]
-GROUPS = [(0, 1), (2, 3), (4, 5), (6,), (7,)]
+PRODUCT_BANKS = 4
+PIECES = [(0, 512), (512, 256), (768, 256)]
+POOL_BLOCK = 0
+GROUPS = [(2, 3), (0, 1), (4, 5), (6,), (7,)]
 
 
 def tile_picked_mixup_gelu_p_kernel(
@@ -36,204 +41,187 @@ def tile_picked_mixup_gelu_p_kernel(
         keep = ctx.enter_context(tc.tile_pool(name="keep", bufs=1))
         psum = ctx.enter_context(tc.psum_pool(name="psum", bufs=1))
 
-        def bank(i, name):
-            return psum.tile([P, 512], F32, name=name, tag="bank%d" % i)
+        def sbuf(shape, dtype, name):
+            return keep.tile(shape, dtype, name=name, align_bytes=ALIGN)
 
-        offs_t = keep.tile([P, S // 16], U16, name="offs_t")
-        nc.sync.dma_start(offs_t[:], offs)
+        def bank(index, name):
+            return psum.tile([P, BANK], F32, name=name, tag="bank%d" % index)
 
-        w1_rows = w1.rearrange("(p j) c -> p j c", j=PACK)
+        def block_bank(b):
+            return PRODUCT_BANKS + b if b < PRODUCT_BANKS else (b + 1) % PRODUCT_BANKS
+
+        def load_scale_rows(plane, rows, queues):
+            for q, queue in enumerate(queues):
+                queue.dma_start(plane[32 * q : 32 * q + 4, :].bitcast(I32), rows[4 * q : 4 * q + 4, :].bitcast(I32))
 
         def load_w1(first, count):
-            raw = keep.tile([P, PACK, P * count], F32, name="w1_raw%d" % first, align_bytes=64)
-            nc.sync.dma_start(raw[:], w1_rows[:, :, P * first : P * (first + count)])
+            raw = sbuf([P, PACK, P * count], F32, "w1_raw%d" % first)
+            rows = w1.rearrange("(p j) c -> p j c", j=PACK)
+            nc.sync.dma_start(raw[:], rows[:, :, P * first : P * (first + count)])
             return raw
 
-
-        xs = keep.tile([P, T], U8, name="xs", tag="xs", align_bytes=64)
-        nc.vector.memset(xs[:, : T // 2].bitcast(I32), 0)
-        nc.gpsimd.memset(xs[:, T // 2 :].bitcast(I32), 0)
-        for q in range(4):
-            (nc.sync if q < 2 else nc.scalar).dma_start(
-                xs[32 * q : 32 * q + 4, :].bitcast(I32),
-                x_scales[0, 4 * q : 4 * q + 4, :].bitcast(I32),
-            )
-
+        offs_t = keep.tile([P, S // PER_COLUMN], U16, name="offs_t")
+        nc.sync.dma_start(offs_t[:], offs)
+        x_plane = sbuf([P, T], U8, "x_plane")
+        nc.vector.memset(x_plane[:, : T // 2].bitcast(I32), 0)
+        nc.gpsimd.memset(x_plane[:, T // 2 :].bitcast(I32), 0)
+        load_scale_rows(x_plane, x_scales[0], [nc.sync, nc.sync, nc.scalar, nc.scalar])
         raw0 = load_w1(0, 1)
-        xw = keep.tile([P, T], I32, name="xw", align_bytes=64)
-        nc.sync.dma_start(xw[:], x_words[0].rearrange("p n t -> p (n t)").bitcast(I32))
+        x_table = sbuf([P, T], I32, "x_table")
+        nc.sync.dma_start(x_table[:], x_words[0].rearrange("p n t -> p (n t)").bitcast(I32))
         raw1, raw23 = load_w1(1, 1), load_w1(2, 2)
-        pos_t = keep.tile([P, S // 16], U16, name="pos_t")
+        pos_t = keep.tile([P, S // PER_COLUMN], U16, name="pos_t")
         nc.sync.dma_start(pos_t[:], pos1)
 
-        ident = keep.tile([P, P], F32, name="ident", align_bytes=64)
+        ident = sbuf([P, P], F32, "ident")
         make_identity(nc, ident[:])
-        warm = keep.tile([P, 2], F32, name="warm")
-        nc.scalar.activation(warm[:], ident[:, 0:2], GELU)
 
-        share_rows = keep.tile([P, P], F32, name="share_rows", align_bytes=64)
+        share_rows = sbuf([P, P], F32, "share_rows")
         nc.gpsimd.memset(share_rows[:], 0.0)
-        w2s = keep.tile([P, N], U8, name="w2s", align_bytes=64)
-        nc.gpsimd.memset(w2s[:].bitcast(I32), 0)
-        nc.sync.dma_start(share_rows[0:8, :], lam[0].rearrange("(b p) -> b p", p=P))
-        nc.sync.dma_start(share_rows[8:16, :], mu[0].rearrange("(b p) -> b p", p=P))
-        w2w = keep.tile([P, 2 * N], U8, name="w2w", align_bytes=64)
-        nc.sync.dma_start(w2w[:].bitcast(I32), w2_words[0].bitcast(I32))
-        for q in range(4):
-            nc.sync.dma_start(
-                w2s[32 * q : 32 * q + 4, :].bitcast(I32),
-                w2_scales[0, 4 * q : 4 * q + 4, :].bitcast(I32),
-            )
+        w2_plane = sbuf([P, N], U8, "w2_plane")
+        nc.gpsimd.memset(w2_plane[:].bitcast(I32), 0)
+        nc.sync.dma_start(share_rows[0:BLOCKS, :], lam[0].rearrange("(b p) -> b p", p=P))
+        nc.sync.dma_start(share_rows[BLOCKS : 2 * BLOCKS, :], mu[0].rearrange("(b p) -> b p", p=P))
+        w2_codes = sbuf([P, 2 * N], U8, "w2_codes")
+        nc.sync.dma_start(w2_codes[:].bitcast(I32), w2_words[0].bitcast(I32))
+        load_scale_rows(w2_plane, w2_scales[0], [nc.sync] * 4)
 
-        xs_g = keep.tile([P, S], U8, name="xs_g", align_bytes=64)
-        nc.vector.tensor_copy(xs_g[:], xs[:].indirect(offs_t[:]))
+        def entries(offsets, first, count):
+            return offsets[:, first // PER_COLUMN : (first + count) // PER_COLUMN]
 
-        def gather_words(dst, lo, n):
-            nc.vector.tensor_copy(dst, xw[:].bitcast(U32).indirect(offs_t[:, lo // 16 : (lo + n) // 16]))
+        def gather_words(dst, piece):
+            nc.vector.tensor_copy(dst, x_table[:].bitcast(U32).indirect(entries(offs_t, *piece)))
             return dst
 
-        def quantize(grouped_flat, width, name):
-            codes = keep.tile([P, width], U32, name=name + "_codes", align_bytes=64)
-            scales = keep.tile([P, width], U8, name=name + "_scales", align_bytes=64)
-            nc.vector.quantize_mx(out=codes[:].bitcast(FP8X4), scales=scales[:], in_=grouped_flat)
+        def quantize(grouped, width, name):
+            codes = sbuf([P, width], U32, name + "_codes")
+            scales = sbuf([P, width], U8, name + "_scales")
+            nc.vector.quantize_mx(out=codes[:].bitcast(FP8X4), scales=scales[:], in_=grouped)
             return codes, scales
 
-        def group_w1(copy, raw, c):
-            grouped = keep.tile([P, raw.shape[2] * PACK], BF16, name="w1_grouped%d" % c, align_bytes=64)
+        def group_w1(copy, raw, name):
+            grouped = sbuf([P, raw.shape[2] * PACK], BF16, name)
             copy(
-                grouped[:].rearrange("p (u m e j) -> p m j u e", u=2, e=2, j=PACK),
-                raw.rearrange("p j (m u e) -> p m j u e", u=2, e=2),
+                grouped[:].rearrange("p (u m e j) -> p u m e j", u=2, e=2, j=PACK),
+                raw[:].rearrange("p j (m u e) -> p u m e j", u=2, e=2),
             )
             return grouped
 
-        pieces = [(0, 512), (512, 256), (768, 256)]
-        xw_a = keep.tile([P, HALF], U32, name="xw_a", align_bytes=64)
-        xw_g = [gather_words(xw_a[:], 0, 512)]
-        grouped0 = group_w1(nc.scalar.copy, raw0[:], 0)
-        q0 = quantize(grouped0[:], P, "w1_0")
-        xw_b = keep.tile([P, HALF], U32, name="xw_b", align_bytes=64)
-        xw_g.append(gather_words(xw_b[:, :256], 512, 256))
-        xw_g.append(gather_words(xw_b[:, 256:], 768, 256))
-        q1 = quantize(group_w1(nc.scalar.copy, raw1[:], 1)[:], P, "w1_1")
-        q23 = quantize(group_w1(nc.vector.tensor_copy, raw23[:], 2)[:], 2 * P, "w1_2")
-        w1q = [q0, q1] + [(q23[0][:, P * u : P * (u + 1)], q23[1][:, P * u : P * (u + 1)]) for u in range(2)]
+        picked_scales = sbuf([P, S], U8, "picked_scales")
+        nc.vector.tensor_copy(picked_scales[:], x_plane[:].indirect(offs_t[:]))
+        words_a = sbuf([P, HALF], U32, "words_a")
+        picked_words = [gather_words(words_a[:], PIECES[0])]
+        w1_0 = quantize(group_w1(nc.scalar.copy, raw0, "w1_grouped0")[:], P, "w1_0")
+        words_b = sbuf([P, HALF], U32, "words_b")
+        picked_words.append(gather_words(words_b[:, : HALF // 2], PIECES[1]))
+        picked_words.append(gather_words(words_b[:, HALF // 2 :], PIECES[2]))
+        w1_1 = quantize(group_w1(nc.scalar.copy, raw1, "w1_grouped1")[:], P, "w1_1")
+        w1_23 = quantize(group_w1(nc.vector.tensor_copy, raw23, "w1_grouped23")[:], 2 * P, "w1_23")
+        w1_tiles = [(w1_0[0][:], w1_0[1][:]), (w1_1[0][:], w1_1[1][:])]
+        w1_tiles.extend((w1_23[0][:, P * u : P * (u + 1)], w1_23[1][:, P * u : P * (u + 1)]) for u in range(2))
 
-        share_ps = bank(7, "share_ps")
-        nc.tensor.transpose(share_ps[:, 0:P], share_rows[:], ident[:])
-        shares = keep.tile([P, 16], F32, name="shares")
-        nc.scalar.copy(shares[:], share_ps[:, 0:16])
+        share_bank = bank(block_bank(PRODUCT_BANKS - 1), "share_bank")
+        nc.tensor.transpose(share_bank[:, 0:P], share_rows[:], ident[:])
+        shares = keep.tile([P, 2 * BLOCKS], F32, name="shares")
+        nc.scalar.copy(shares[:], share_bank[:, 0 : 2 * BLOCKS])
 
-        def cols(bk, c):
-            if c < 2:
-                return bk[:].rearrange("p (u c r) -> p c u r", u=2, c=4)[:, c]
-            return bk[:, 256 * (c - 2) + P : 256 * (c - 1)]
-
-        h = []
-        g = {}
-        g_tag = {}
-        steps = [(0, [0]), (0, [1]), (0, [2])] + [(c, ids) for c in range(1, 4) for ids in ([0], [1, 2])]
-        for c in range(4):
-            h.append(keep.tile([P, S], F32, name="h%d" % c, tag="h%d" % c, align_bytes=64))
+        steps = [(0, [0]), (0, [1]), (0, [2])] + [(c, ids) for c in range(1, TILES) for ids in ([0], [1, 2])]
+        h = [sbuf([P, S], F32, "h%d" % c) for c in range(TILES)]
         for k, (c, ids) in enumerate(steps):
-            acc = bank(ACC_BANK[k], "acc%d_%d" % (c, ids[0]))
-            first = pieces[ids[0]][0]
-            width = sum(pieces[i][1] for i in ids)
+            acc = bank(k % PRODUCT_BANKS, "acc%d" % k)
+            first = PIECES[ids[0]][0]
+            width = sum(PIECES[i][1] for i in ids)
             for i in ids:
-                lo, n = pieces[i]
+                lo, count = PIECES[i]
                 nc.tensor.matmul_mx(
-                    out=acc[:, lo - first : lo - first + n],
-                    lhsT=w1q[c][0][:].bitcast(FP8X4),
-                    lhsT_scale=w1q[c][1][:],
-                    rhs=xw_g[i].bitcast(FP8X4),
-                    rhs_scale=xs_g[:, lo : lo + n],
+                    out=acc[:, lo - first : lo - first + count],
+                    lhsT=w1_tiles[c][0].bitcast(FP8X4),
+                    lhsT_scale=w1_tiles[c][1],
+                    rhs=picked_words[i].bitcast(FP8X4),
+                    rhs_scale=picked_scales[:, lo : lo + count],
                     start=True,
                     stop=True,
                 )
             nc.scalar.activation(h[c][:, first : first + width], acc[:, :width], GELU)
 
-        def bank_of(b):
-            return BLOCK_BANK[b]
+        def turn(dst, c, src):
+            if c < 2:
+                columns = dst[:].rearrange("p (u c r) -> p c u r", u=2, c=TILES)[:, c]
+            else:
+                columns = dst[:, 256 * (c - 2) + P : 256 * (c - 1)]
+            nc.tensor.transpose(columns, src, ident[:])
 
-        hT = [bank(bank_of(b), "hT%d" % b) for b in range(BLOCKS)]
         def ready_step(c, b):
-            made = max(k for k, (cc, ids) in enumerate(steps) if cc == c and pieces[ids[0]][0] <= P * b)
-            freed = max([k for k in range(len(steps)) if ACC_BANK[k] == bank_of(b)] + [0])
+            made = max(k for k, (tile, ids) in enumerate(steps) if tile == c and PIECES[ids[0]][0] <= P * b)
+            freed = max([k for k in range(len(steps)) if k % PRODUCT_BANKS == block_bank(b)] + [0])
             return max(made, freed)
 
-        order = sorted((ready_step(c, b), b, c) for b in range(BLOCKS) for c in range(4))
-        order = [(c, b) for step, b, c in order]
-        for c, b in order:
-            nc.tensor.transpose(cols(hT[b], c), h[c][:, P * b : P * (b + 1)], ident[:])
-
-        def gather_h(c, hf):
-            name = "g%d_%d" % (c, hf)
-            gt = keep.tile([P, HALF], F32, name=name, tag=g_tag.get((c, hf), name), align_bytes=64)
-            nc.vector.tensor_copy(gt[:], h[c][:].indirect(pos_t[:, 32 * hf : 32 * (hf + 1)]))
-            g[c, hf] = gt
-
-        own = []
+        h_turned = [bank(block_bank(b), "h_turned%d" % b) for b in range(BLOCKS)]
+        for step, b, c in sorted((ready_step(c, b), b, c) for b in range(BLOCKS) for c in range(TILES)):
+            turn(h_turned[b], c, h[c][:, P * b : P * (b + 1)])
+        own = [sbuf([P, H], F32, "own%d" % b) for b in range(BLOCKS)]
         for b in range(BLOCKS):
-            a = keep.tile([P, H], F32, name="own%d" % b, tag="own%d" % b, align_bytes=64)
-            nc.scalar.activation(a[:], hT[b][:], COPY, scale=shares[:, b : b + 1])
-            own.append(a)
+            nc.scalar.activation(own[b][:], h_turned[b][:], COPY, scale=shares[:, b : b + 1])
 
-        gT = [bank(bank_of(b), "gT%d" % b) for b in range(BLOCKS)]
-        for c in range(4):
-            for hf in range(2):
-                gather_h(c, hf)
+        partners = {}
+        for c in range(TILES):
+            for half in range(2):
+                partners[c, half] = sbuf([P, HALF], F32, "partners%d_%d" % (c, half))
+                nc.vector.tensor_copy(partners[c, half][:], h[c][:].indirect(entries(pos_t, HALF * half, HALF)))
 
-        def turn_g(c, b):
-            nc.tensor.transpose(cols(gT[b], c), g[c, b // 4][:, P * (b % 4) : P * (b % 4 + 1)], ident[:])
-
-        order = [(c, b) for b in range(4) for c in range(2)] + [(2, b) for b in range(4)]
-        order = order + [(c, b) for b in range(4, 7) for c in range(3)] + [(3, b) for b in range(4)]
-        order = order + [(c, 7) for c in range(3)] + [(3, b) for b in range(4, 8)]
+        mix_order = [POOL_BLOCK] + [b for group in GROUPS for b in group if b != POOL_BLOCK]
+        first_half = [b for b in mix_order if b < BLOCKS // 2]
+        last = BLOCKS - 1
+        order = [(c, b) for b in range(BLOCKS // 2) for c in (0, 1)] + [(2, b) for b in range(BLOCKS // 2)]
+        order = order + [(c, b) for b in range(BLOCKS // 2, last) for c in (0, 1, 2)] + [(3, b) for b in first_half]
+        order = order + [(c, last) for c in (0, 1, 2)] + [(3, b) for b in range(BLOCKS // 2, BLOCKS)]
+        p_turned = [bank(block_bank(b), "p_turned%d" % b) for b in range(BLOCKS)]
         for c, b in order:
-            turn_g(c, b)
+            half, place = divmod(b, BLOCKS // 2)
+            turn(p_turned[b], c, partners[c, half][:, P * place : P * (place + 1)])
 
-        zT = {}
+        mixed = {}
+        for b in mix_order:
+            mixed[b] = sbuf([P, H], BF16, "mixed%d" % b)
+            mu_b = shares[:, BLOCKS + b : BLOCKS + b + 1]
+            if b == POOL_BLOCK:
+                scaled = sbuf([P, H], F32, "scaled")
+                nc.scalar.activation(scaled[:], p_turned[b][:], COPY, scale=mu_b)
+                nc.gpsimd.tensor_tensor(mixed[b][:], scaled[:], own[b][:], ADD)
+            else:
+                nc.vector.scalar_tensor_tensor(mixed[b][:], p_turned[b][:], mu_b, own[b][:], MULT, ADD)
 
-        def mix(b):
-            z = keep.tile([P, H], BF16, name="zT%d" % b, align_bytes=64)
-            nc.vector.scalar_tensor_tensor(z[:], gT[b][:], shares[:, 8 + b : 9 + b], own[b][:], MULT, ADD)
-            zT[b] = z
-
-        def turn(grp):
-            n = P * len(grp)
-            wb = bank(bank_of(grp[0]), "words%d" % grp[0])
-            for i, b in enumerate(grp):
-                words = zT[b][:].bitcast(F32)
+        z_grouped = []
+        for group in GROUPS:
+            count = P * len(group)
+            pair_bank = bank(block_bank(group[0]), "pairs%d" % group[0])
+            for i, b in enumerate(group):
+                pairs = mixed[b][:].bitcast(F32)
                 for u in range(2):
-                    nc.tensor.transpose(
-                        wb[:, 256 * i + P * u : 256 * i + P * (u + 1)], words[:, P * u : P * (u + 1)], ident[:]
-                    )
-            zg = keep.tile([P, n, PACK], BF16, name="zg%d" % grp[0], align_bytes=64)
-            dst = zg[:].rearrange("p s t -> p (s t)").bitcast(F32).rearrange("p (i s u) -> p i s u", u=2, s=P)
-            nc.scalar.copy(dst, wb[:, 0 : 2 * n].rearrange("p (i u s) -> p i s u", u=2, s=P))
-            return zg
+                    column = P * (2 * i + u)
+                    nc.tensor.transpose(pair_bank[:, column : column + P], pairs[:, P * u : P * (u + 1)], ident[:])
+            grouped = sbuf([P, count * PACK], BF16, "z_grouped%d" % group[0])
+            nc.scalar.copy(
+                grouped[:].bitcast(F32).rearrange("p (i s u) -> p i s u", u=2, s=P),
+                pair_bank[:, 0 : 2 * count].rearrange("p (i u s) -> p i s u", u=2, s=P),
+            )
+            z_grouped.append(grouped)
 
-        def finish(grp, zg, ob):
-            n = P * len(grp)
-            codes, scales = quantize(zg[:].rearrange("p s t -> p (s t)"), n, "z%d" % grp[0])
-            acc = bank(ob, "out%d" % grp[0])
+        out_banks = [block_bank(group[1]) for group in GROUPS[:3]] + [block_bank(group[0]) for group in GROUPS[:2]]
+        for group, grouped, out_bank in zip(GROUPS, z_grouped, out_banks):
+            count = P * len(group)
+            codes, scales = quantize(grouped[:], count, "z%d" % group[0])
+            acc = bank(out_bank, "out%d" % group[0])
             nc.tensor.matmul_mx(
-                out=acc[:, 0:n],
-                lhsT=w2w[:].bitcast(FP4X4),
-                lhsT_scale=w2s[:],
+                out=acc[:, 0:count],
+                lhsT=w2_codes[:].bitcast(FP4X4),
+                lhsT_scale=w2_plane[:],
                 rhs=codes[:].bitcast(FP8X4),
                 rhs_scale=scales[:],
                 start=True,
                 stop=True,
             )
-            res = keep.tile([P, n], F32, name="res%d" % grp[0], align_bytes=64)
-            (nc.vector.tensor_copy if grp[0] == 7 else nc.scalar.copy)(res[:], acc[:, 0:n])
-            nc.sync.dma_start(out[:, P * grp[0] : P * grp[0] + n], res[:])
-
-        out_banks = [bank_of(1), bank_of(3), bank_of(5), bank_of(0), bank_of(2)]
-        turned = []
-        for grp in GROUPS:
-            for b in grp:
-                mix(b)
-            turned.append(turn(grp))
-        for grp, zg, ob in zip(GROUPS, turned, out_banks):
-            finish(grp, zg, ob)
+            result = sbuf([P, count], F32, "result%d" % group[0])
+            copy = nc.vector.tensor_copy if group == GROUPS[-1] else nc.scalar.copy
+            copy(result[:], acc[:, 0:count])
+            nc.sync.dma_start(out[:, P * group[0] : P * group[0] + count], result[:])

from contextlib import ExitStack

import concourse.mybir as mybir
from concourse.masks import make_identity

K, T, S, H, N = 512, 2048, 1024, 512, 128
FLOPS = 2 * K * H * S + 2 * H * N * S

F32 = mybir.dt.float32
BF16 = mybir.dt.bfloat16
I32 = mybir.dt.int32
U32 = mybir.dt.uint32
U16 = mybir.dt.uint16
U8 = mybir.dt.uint8
FP8X4 = mybir.dt.float8_e4m3fn_x4
FP4X4 = mybir.dt.float4_e2m1fn_x4
GELU = mybir.ActivationFunctionType.Gelu_apprx_tanh
COPY = mybir.ActivationFunctionType.Copy
MULT = mybir.AluOpType.mult
ADD = mybir.AluOpType.add

P = 128
PACK = 4
ALIGN = 64
BANK = 512
HALF = S // 2
PER_COLUMN = 16
TILES = H // P
BLOCKS = S // P
PRODUCT_BANKS = 4
PIECES = [(0, 512), (512, 256), (768, 256)]
POOL_BLOCK = 0
GROUPS = [(2, 3), (0, 1), (4, 5), (6,), (7,)]


def tile_picked_mixup_gelu_p_kernel(
    tc, x_words, x_scales, w1, w2_words, w2_scales, lam, mu, offs, pos1, out
):
    nc = tc.nc
    with ExitStack() as ctx:
        keep = ctx.enter_context(tc.tile_pool(name="keep", bufs=1))
        psum = ctx.enter_context(tc.psum_pool(name="psum", bufs=1))

        def sbuf(shape, dtype, name):
            return keep.tile(shape, dtype, name=name, align_bytes=ALIGN)

        def bank(index, name):
            return psum.tile([P, BANK], F32, name=name, tag="bank%d" % index)

        def block_bank(b):
            return PRODUCT_BANKS + b if b < PRODUCT_BANKS else (b + 1) % PRODUCT_BANKS

        def load_scale_rows(plane, rows, queues):
            for q, queue in enumerate(queues):
                queue.dma_start(plane[32 * q : 32 * q + 4, :].bitcast(I32), rows[4 * q : 4 * q + 4, :].bitcast(I32))

        def load_w1(first, count):
            raw = sbuf([P, PACK, P * count], F32, "w1_raw%d" % first)
            rows = w1.rearrange("(p j) c -> p j c", j=PACK)
            nc.sync.dma_start(raw[:], rows[:, :, P * first : P * (first + count)])
            return raw

        offs_t = keep.tile([P, S // PER_COLUMN], U16, name="offs_t")
        nc.sync.dma_start(offs_t[:], offs)
        x_plane = sbuf([P, T], U8, "x_plane")
        nc.vector.memset(x_plane[:, : T // 2].bitcast(I32), 0)
        nc.gpsimd.memset(x_plane[:, T // 2 :].bitcast(I32), 0)
        load_scale_rows(x_plane, x_scales[0], [nc.sync, nc.sync, nc.scalar, nc.scalar])
        raw0 = load_w1(0, 1)
        x_table = sbuf([P, T], I32, "x_table")
        nc.sync.dma_start(x_table[:], x_words[0].rearrange("p n t -> p (n t)").bitcast(I32))
        raw1, raw23 = load_w1(1, 1), load_w1(2, 2)
        pos_t = keep.tile([P, S // PER_COLUMN], U16, name="pos_t")
        nc.sync.dma_start(pos_t[:], pos1)

        ident = sbuf([P, P], F32, "ident")
        make_identity(nc, ident[:])

        share_rows = sbuf([P, P], F32, "share_rows")
        nc.gpsimd.memset(share_rows[:], 0.0)
        w2_plane = sbuf([P, N], U8, "w2_plane")
        nc.gpsimd.memset(w2_plane[:].bitcast(I32), 0)
        nc.sync.dma_start(share_rows[0:BLOCKS, :], lam[0].rearrange("(b p) -> b p", p=P))
        nc.sync.dma_start(share_rows[BLOCKS : 2 * BLOCKS, :], mu[0].rearrange("(b p) -> b p", p=P))
        w2_codes = sbuf([P, 2 * N], U8, "w2_codes")
        nc.sync.dma_start(w2_codes[:].bitcast(I32), w2_words[0].bitcast(I32))
        load_scale_rows(w2_plane, w2_scales[0], [nc.sync] * 4)

        def entries(offsets, first, count):
            return offsets[:, first // PER_COLUMN : (first + count) // PER_COLUMN]

        def gather_words(dst, piece):
            nc.vector.tensor_copy(dst, x_table[:].bitcast(U32).indirect(entries(offs_t, *piece)))
            return dst

        def quantize(grouped, width, name):
            codes = sbuf([P, width], U32, name + "_codes")
            scales = sbuf([P, width], U8, name + "_scales")
            nc.vector.quantize_mx(out=codes[:].bitcast(FP8X4), scales=scales[:], in_=grouped)
            return codes, scales

        def group_w1(copy, raw, name):
            grouped = sbuf([P, raw.shape[2] * PACK], BF16, name)
            copy(
                grouped[:].rearrange("p (u m e j) -> p u m e j", u=2, e=2, j=PACK),
                raw[:].rearrange("p j (m u e) -> p u m e j", u=2, e=2),
            )
            return grouped

        picked_scales = sbuf([P, S], U8, "picked_scales")
        nc.vector.tensor_copy(picked_scales[:], x_plane[:].indirect(offs_t[:]))
        words_a = sbuf([P, HALF], U32, "words_a")
        picked_words = [gather_words(words_a[:], PIECES[0])]
        w1_0 = quantize(group_w1(nc.scalar.copy, raw0, "w1_grouped0")[:], P, "w1_0")
        words_b = sbuf([P, HALF], U32, "words_b")
        picked_words.append(gather_words(words_b[:, : HALF // 2], PIECES[1]))
        picked_words.append(gather_words(words_b[:, HALF // 2 :], PIECES[2]))
        w1_1 = quantize(group_w1(nc.scalar.copy, raw1, "w1_grouped1")[:], P, "w1_1")
        w1_23 = quantize(group_w1(nc.vector.tensor_copy, raw23, "w1_grouped23")[:], 2 * P, "w1_23")
        w1_tiles = [(w1_0[0][:], w1_0[1][:]), (w1_1[0][:], w1_1[1][:])]
        w1_tiles.extend((w1_23[0][:, P * u : P * (u + 1)], w1_23[1][:, P * u : P * (u + 1)]) for u in range(2))

        share_bank = bank(block_bank(PRODUCT_BANKS - 1), "share_bank")
        nc.tensor.transpose(share_bank[:, 0:P], share_rows[:], ident[:])
        shares = keep.tile([P, 2 * BLOCKS], F32, name="shares")
        nc.scalar.copy(shares[:], share_bank[:, 0 : 2 * BLOCKS])

        steps = [(0, [0]), (0, [1]), (0, [2])] + [(c, ids) for c in range(1, TILES) for ids in ([0], [1, 2])]
        h = [sbuf([P, S], F32, "h%d" % c) for c in range(TILES)]
        for k, (c, ids) in enumerate(steps):
            acc = bank(k % PRODUCT_BANKS, "acc%d" % k)
            first = PIECES[ids[0]][0]
            width = sum(PIECES[i][1] for i in ids)
            for i in ids:
                lo, count = PIECES[i]
                nc.tensor.matmul_mx(
                    out=acc[:, lo - first : lo - first + count],
                    lhsT=w1_tiles[c][0].bitcast(FP8X4),
                    lhsT_scale=w1_tiles[c][1],
                    rhs=picked_words[i].bitcast(FP8X4),
                    rhs_scale=picked_scales[:, lo : lo + count],
                    start=True,
                    stop=True,
                )
            nc.scalar.activation(h[c][:, first : first + width], acc[:, :width], GELU)

        def turn(dst, c, src):
            if c < 2:
                columns = dst[:].rearrange("p (u c r) -> p c u r", u=2, c=TILES)[:, c]
            else:
                columns = dst[:, 256 * (c - 2) + P : 256 * (c - 1)]
            nc.tensor.transpose(columns, src, ident[:])

        def ready_step(c, b):
            made = max(k for k, (tile, ids) in enumerate(steps) if tile == c and PIECES[ids[0]][0] <= P * b)
            freed = max([k for k in range(len(steps)) if k % PRODUCT_BANKS == block_bank(b)] + [0])
            return max(made, freed)

        h_turned = [bank(block_bank(b), "h_turned%d" % b) for b in range(BLOCKS)]
        for step, b, c in sorted((ready_step(c, b), b, c) for b in range(BLOCKS) for c in range(TILES)):
            turn(h_turned[b], c, h[c][:, P * b : P * (b + 1)])
        own = [sbuf([P, H], F32, "own%d" % b) for b in range(BLOCKS)]
        for b in range(BLOCKS):
            nc.scalar.activation(own[b][:], h_turned[b][:], COPY, scale=shares[:, b : b + 1])

        partners = {}
        for c in range(TILES):
            for half in range(2):
                partners[c, half] = sbuf([P, HALF], F32, "partners%d_%d" % (c, half))
                nc.vector.tensor_copy(partners[c, half][:], h[c][:].indirect(entries(pos_t, HALF * half, HALF)))

        mix_order = [POOL_BLOCK] + [b for group in GROUPS for b in group if b != POOL_BLOCK]
        first_half = [b for b in mix_order if b < BLOCKS // 2]
        last = BLOCKS - 1
        order = [(c, b) for b in range(BLOCKS // 2) for c in (0, 1)] + [(2, b) for b in range(BLOCKS // 2)]
        order = order + [(c, b) for b in range(BLOCKS // 2, last) for c in (0, 1, 2)] + [(3, b) for b in first_half]
        order = order + [(c, last) for c in (0, 1, 2)] + [(3, b) for b in range(BLOCKS // 2, BLOCKS)]
        p_turned = [bank(block_bank(b), "p_turned%d" % b) for b in range(BLOCKS)]
        for c, b in order:
            half, place = divmod(b, BLOCKS // 2)
            turn(p_turned[b], c, partners[c, half][:, P * place : P * (place + 1)])

        mixed = {}
        for b in mix_order:
            mixed[b] = sbuf([P, H], BF16, "mixed%d" % b)
            mu_b = shares[:, BLOCKS + b : BLOCKS + b + 1]
            if b == POOL_BLOCK:
                scaled = sbuf([P, H], F32, "scaled")
                nc.scalar.activation(scaled[:], p_turned[b][:], COPY, scale=mu_b)
                nc.gpsimd.tensor_tensor(mixed[b][:], scaled[:], own[b][:], ADD)
            else:
                nc.vector.scalar_tensor_tensor(mixed[b][:], p_turned[b][:], mu_b, own[b][:], MULT, ADD)

        z_grouped = []
        for group in GROUPS:
            count = P * len(group)
            pair_bank = bank(block_bank(group[0]), "pairs%d" % group[0])
            for i, b in enumerate(group):
                pairs = mixed[b][:].bitcast(F32)
                for u in range(2):
                    column = P * (2 * i + u)
                    nc.tensor.transpose(pair_bank[:, column : column + P], pairs[:, P * u : P * (u + 1)], ident[:])
            grouped = sbuf([P, count * PACK], BF16, "z_grouped%d" % group[0])
            nc.scalar.copy(
                grouped[:].bitcast(F32).rearrange("p (i s u) -> p i s u", u=2, s=P),
                pair_bank[:, 0 : 2 * count].rearrange("p (i u s) -> p i s u", u=2, s=P),
            )
            z_grouped.append(grouped)

        out_banks = [block_bank(group[1]) for group in GROUPS[:3]] + [block_bank(group[0]) for group in GROUPS[:2]]
        for group, grouped, out_bank in zip(GROUPS, z_grouped, out_banks):
            count = P * len(group)
            codes, scales = quantize(grouped[:], count, "z%d" % group[0])
            acc = bank(out_bank, "out%d" % group[0])
            nc.tensor.matmul_mx(
                out=acc[:, 0:count],
                lhsT=w2_codes[:].bitcast(FP4X4),
                lhsT_scale=w2_plane[:],
                rhs=codes[:].bitcast(FP8X4),
                rhs_scale=scales[:],
                start=True,
                stop=True,
            )
            result = sbuf([P, count], F32, "result%d" % group[0])
            copy = nc.vector.tensor_copy if group == GROUPS[-1] else nc.scalar.copy
            copy(result[:], acc[:, 0:count])
            nc.sync.dma_start(out[:, P * group[0] : P * group[0] + count], result[:])
